import numpy as np, ml_dtypes
CORES = [6,14,22,30,38,134,142,150,158]
N = 9
WB, KB, QP = 1, 4, 64
def setup_inputs(rng):
    return {"q": rng.standard_normal((N, 128, QP), dtype=np.float32).astype(ml_dtypes.bfloat16), "k": rng.standard_normal((N, 128, KB * 128), dtype=np.float32).astype(ml_dtypes.bfloat16), "v": rng.standard_normal((N, 128, KB * 128), dtype=np.float32).astype(ml_dtypes.bfloat16)}
def setup_inputs_big(rng):
    d = setup_inputs(rng)
    for k in ("q", "k", "v"): d[k] = (d[k].astype(np.float32) * 1024.0).astype(d[k].dtype)
    return d
def setup_inputs_small(rng):
    d = setup_inputs(rng)
    for k in ("q", "k", "v"): d[k] = (d[k].astype(np.float32) * (1 / 1024.0)).astype(d[k].dtype)
    return d
def setup_inputs_apart(rng):
    d = setup_inputs(rng)
    f = (10.0 ** rng.permutation(np.linspace(-1.5, 1.5, N))).astype(np.float32).reshape(N, 1, 1)
    for k in ("q", "k", "v"): d[k] = (d[k].astype(np.float32) * f).astype(d[k].dtype)
    return d
def reference(q, k, v):
    Q, K, V = q.astype(np.float64), k.astype(np.float64), v.astype(np.float64)
    y = np.zeros((N, 128, QP))
    for r in range(N):
        for j in range(max(0, r - WB), r + 1):
            for b in range(KB):
                S = np.maximum(K[j][:, 128 * b:128 * b + 128].T @ Q[r], 0.0)
                y[r] += V[j][:, 128 * b:128 * b + 128].T @ S
    return {"y": y.astype(ml_dtypes.bfloat16 if q.dtype != np.float64 else np.float64)}

@@ -1,0 +1,141 @@
+from concourse.mybir import AluOpType
+
+P = 128
+KB, QP = 4, 64
+KW = KB * P
+NENG = 8
+
+SCRATCH = {
+    "qs":   ("sbuf", [P, QP], "bfloat16"),
+    "kv":   ("sbuf", [P, 2 * KW], "bfloat16"),
+    "qn":   ("sbuf", [P, QP], "bfloat16"),
+    "kvx":  ("sbuf", [P, 2 * P], "bfloat16"),
+    "pl":   ("sbuf", [P, QP], "bfloat16"),
+    "ps":   ("sbuf", [P, QP], "bfloat16"),
+    "zero": ("sbuf", [P, (KB + 1) * QP], "float32"),
+    "sn":   ("sbuf", [P, KB * QP], "bfloat16"),
+    "sw":   ("sbuf", [P, (KB + 1) * QP], "bfloat16"),
+    "yb":   ("sbuf", [P, QP], "bfloat16"),
+    "pna":  ("psum", [P, 512], "float32"),
+    "pnb":  ("psum", [P, 512], "float32"),
+    "pno":  ("psum", [P, 512], "float32"),
+    "pws":  ("psum", [P, 512], "float32"),
+    "pwo":  ("psum", [P, 512], "float32"),
+}
+SEMAPHORES = ["qld", "qiss", "kld", "vld", "shld", "qarr", "xarr", "parr", "sent", "zs",
+              "sna", "snb", "rna", "rnb", "ono", "cpn", "sws", "rws", "owo", "fin", "yst"]
+
+
+def _engines(mask, n):
+    bits = [i for i in range(mask.bit_length()) if (mask >> i) & 1][:n]
+    return sum(1 << i for i in bits)
+
+
+def rank_program(g, core, T, topo):
+    r = T.rank_of(core)
+    if r is None:
+        return
+    cores = T.cores
+    prev = cores[r - 1] if r > 0 else None
+    nxt = cores[r + 1] if r + 1 < len(cores) else None
+    S = T.sem
+    ships = prev is None and nxt is not None
+    gets = prev is not None and T.rank_of(prev) == 0
+    sb = KB - 1
+
+    def kcol(b):
+        return P * b
+
+    def vcol(b):
+        return KW + P * ((b + 1) % KB) if ships else KW + P * b
+
+    sent = [0]
+
+    def send(dst, out_ap, in_ap, sem):
+        rid, pid = topo.addr(dst, core)
+        g.remote_dma(out_ap=out_ap, in_ap=in_ap, remote_sem=sem, local_sem=S.sent, pid=pid, routing_id=rid,
+                     dma_engine_mask=_engines(topo.mask(core, dst), NENG))
+        sent[0] += NENG
+
+    if ships:
+        g.sync.dma_start(T.kv[:, kcol(sb):kcol(sb) + P], T.k[:, P * sb:P * sb + P]).then_inc(S.shld, 16)
+        g.scalar.dma_start(T.kv[:, vcol(sb):vcol(sb) + P], T.v[:, P * sb:P * sb + P]).then_inc(S.shld, 16)
+        g.sync.dma_start(T.kv[:, 0:P * sb], T.k[:, 0:P * sb]).then_inc(S.kld, 16)
+        g.scalar.dma_start(T.kv[:, vcol(0):vcol(0) + P * sb], T.v[:, 0:P * sb]).then_inc(S.vld, 16)
+        g.sync.dma_start(T.qs[:], T.q[:]).then_inc(S.qld, 16)
+    else:
+        g.sync.dma_start(T.qs[:], T.q[:]).then_inc(S.qld, 16)
+        g.sync.sem_inc(S.qiss, 1)
+        g.sync.dma_start(T.kv[:, 0:KW], T.k[:]).then_inc(S.kld, 16)
+        g.scalar.wait_ge(S.qiss, 1)
+        g.scalar.dma_start(T.kv[:, KW:2 * KW], T.v[:]).then_inc(S.vld, 16)
+
+    if ships:
+        g.wait_ge(S.shld, 32)
+        send(nxt, T.kvx[:], T.kv[:, kcol(sb):kcol(sb) + 2 * P], S.xarr)
+    if prev is not None:
+        g.wait_ge(S.qld, 16)
+        send(prev, T.qn[:], T.qs[:], S.qarr)
+    if nxt is not None:
+        g.wait_ge(S.cpn, 1)
+        send(nxt, T.pl[:], T.ps[:], S.parr)
+    if sent[0]:
+        g.wait_ge(S.sent, sent[0])
+
+    nb = [b for b in range(KB) if not (ships and b == sb)] if nxt is not None else []
+    half = (len(nb) + 1) // 2
+    own = [(T.kv[:, kcol(b):kcol(b) + P], T.kv[:, vcol(b):vcol(b) + P]) for b in range(KB)]
+    if gets:
+        own.append((T.kvx[:, 0:P], T.kvx[:, P:2 * P]))
+
+    te, ve = g.tensor, g.vector
+
+    te.wait_ge(S.kld, 16)
+    if nb:
+        te.wait_ge(S.qarr, NENG)
+        for i, b in enumerate(nb):
+            bank, sem, c = (T.pna, S.sna, i) if i < half else (T.pnb, S.snb, i - half)
+            te.matmul(bank[:, c * QP:(c + 1) * QP], T.kv[:, kcol(b):kcol(b) + P], T.qn[:], True, True).then_inc(sem, 1)
+        te.wait_ge(S.vld, 16)
+        te.wait_ge(S.rna, 1)
+        for i, b in enumerate(nb):
+            if i == half:
+                te.wait_ge(S.rnb, 1)
+            te.matmul(T.pno[:, 0:QP], T.kv[:, vcol(b):vcol(b) + P], T.sn[:, i * QP:(i + 1) * QP],
+                      i == 0, i == len(nb) - 1).then_inc(S.ono, 1)
+    else:
+        te.wait_ge(S.vld, 16)
+    te.wait_ge(S.qld, 16)
+    if ships:
+        te.wait_ge(S.shld, 32)
+    if gets:
+        te.wait_ge(S.xarr, NENG)
+    for i, (kb, vb) in enumerate(own):
+        te.matmul(T.pws[:, i * QP:(i + 1) * QP], kb, T.qs[:], True, True).then_inc(S.sws, 1)
+    te.wait_ge(S.rws, 1)
+    for i, (kb, vb) in enumerate(own):
+        te.matmul(T.pwo[:, 0:QP], vb, T.sw[:, i * QP:(i + 1) * QP], i == 0, i == len(own) - 1).then_inc(S.owo, 1)
+
+    ve.memset(T.zero[:], 0.0).then_inc(S.zs, 1)
+    ve.wait_ge(S.zs, 1)
+    if nb:
+        wa, wb = half * QP, (len(nb) - half) * QP
+        ve.wait_ge(S.sna, half)
+        ve.tensor_tensor(T.sn[:, 0:wa], T.pna[:, 0:wa], T.zero[:, 0:wa], AluOpType.max).then_inc(S.rna, 1)
+        ve.wait_ge(S.snb, len(nb) - half)
+        ve.tensor_tensor(T.sn[:, wa:wa + wb], T.pnb[:, 0:wb], T.zero[:, 0:wb], AluOpType.max).then_inc(S.rnb, 1)
+        ve.wait_ge(S.ono, len(nb))
+        ve.tensor_copy(T.ps[:], T.pno[:, 0:QP]).then_inc(S.cpn, 1)
+    ww = len(own) * QP
+    ve.wait_ge(S.sws, len(own))
+    ve.tensor_tensor(T.sw[:, 0:ww], T.pws[:, 0:ww], T.zero[:, 0:ww], AluOpType.max).then_inc(S.rws, 1)
+    ve.wait_ge(S.owo, len(own))
+    if prev is not None:
+        ve.wait_ge(S.parr, NENG)
+        ve.tensor_tensor(T.yb[:], T.pwo[:, 0:QP], T.pl[:], AluOpType.add).then_inc(S.fin, 1)
+    else:
+        ve.tensor_copy(T.yb[:], T.pwo[:, 0:QP]).then_inc(S.fin, 1)
+
+    g.sync.wait_ge(S.fin, 1)
+    g.sync.dma_start(T.y[:], T.yb[:]).then_inc(S.yst, 16)
+    g.sync.wait_ge(S.yst, 16)

@@ -3,32 +3,38 @@ from concourse.mybir import AluOpType
 P = 128
 KB, QP = 4, 64
 KW = KB * P
-NENG = 8
+HB = KB // 2
+HW = HB * QP
 
 SCRATCH = {
     "qs":   ("sbuf", [P, QP], "bfloat16"),
     "kv":   ("sbuf", [P, 2 * KW], "bfloat16"),
     "qn":   ("sbuf", [P, QP], "bfloat16"),
+    "wl":   ("sbuf", [P, QP], "bfloat16"),
     "kvx":  ("sbuf", [P, 2 * P], "bfloat16"),
     "pl":   ("sbuf", [P, QP], "bfloat16"),
     "ps":   ("sbuf", [P, QP], "bfloat16"),
-    "zero": ("sbuf", [P, (KB + 1) * QP], "float32"),
+    "wb":   ("sbuf", [P, QP], "bfloat16"),
+    "zero": ("sbuf", [P, HW], "float32"),
     "sn":   ("sbuf", [P, KB * QP], "bfloat16"),
     "sw":   ("sbuf", [P, (KB + 1) * QP], "bfloat16"),
     "yb":   ("sbuf", [P, QP], "bfloat16"),
-    "pna":  ("psum", [P, 512], "float32"),
-    "pnb":  ("psum", [P, 512], "float32"),
+    "pn0":  ("psum", [P, 512], "float32"),
+    "pn1":  ("psum", [P, 512], "float32"),
+    "pn2":  ("psum", [P, 512], "float32"),
+    "pn3":  ("psum", [P, 512], "float32"),
     "pno":  ("psum", [P, 512], "float32"),
-    "pws":  ("psum", [P, 512], "float32"),
+    "pwa":  ("psum", [P, 512], "float32"),
+    "pwb":  ("psum", [P, 512], "float32"),
     "pwo":  ("psum", [P, 512], "float32"),
 }
-SEMAPHORES = ["qld", "qiss", "kld", "vld", "shld", "qarr", "xarr", "parr", "sent", "zs",
-              "sna", "snb", "rna", "rnb", "ono", "cpn", "sws", "rws", "owo", "fin", "yst"]
+SEMAPHORES = ["qld", "qiss", "kld", "vld", "shld", "qarr", "warr", "xarr", "parr", "sent", "zs",
+              "sn0", "sn1", "sn2", "sn3", "rn0", "rn1", "rn2", "rn3", "ono", "cpn", "wcp",
+              "swa", "swb", "rwa", "rwb", "sxs", "rxs", "owo", "fin", "yst"]
 
 
-def _engines(mask, n):
-    bits = [i for i in range(mask.bit_length()) if (mask >> i) & 1][:n]
-    return sum(1 << i for i in bits)
+def _count(mask):
+    return sum((mask >> i) & 1 for i in range(mask.bit_length()))
 
 
 def rank_program(g, core, T, topo):
@@ -41,6 +47,8 @@ def rank_program(g, core, T, topo):
     S = T.sem
     ships = prev is None and nxt is not None
     gets = prev is not None and T.rank_of(prev) == 0
+    whole = prev is not None and not gets
+    gives = nxt is not None and not ships
     sb = KB - 1
 
     def kcol(b):
@@ -53,9 +61,13 @@ def rank_program(g, core, T, topo):
 
     def send(dst, out_ap, in_ap, sem):
         rid, pid = topo.addr(dst, core)
+        mask = topo.mask(core, dst)
         g.remote_dma(out_ap=out_ap, in_ap=in_ap, remote_sem=sem, local_sem=S.sent, pid=pid, routing_id=rid,
-                     dma_engine_mask=_engines(topo.mask(core, dst), NENG))
-        sent[0] += NENG
+                     dma_engine_mask=mask)
+        sent[0] += _count(mask)
+
+    nfrom_prev = _count(topo.mask(prev, core)) if prev is not None else 0
+    nfrom_next = _count(topo.mask(nxt, core)) if nxt is not None else 0
 
     if ships:
         g.sync.dma_start(T.kv[:, kcol(sb):kcol(sb) + P], T.k[:, P * sb:P * sb + P]).then_inc(S.shld, 16)
@@ -76,6 +88,9 @@ def rank_program(g, core, T, topo):
     if prev is not None:
         g.wait_ge(S.qld, 16)
         send(prev, T.qn[:], T.qs[:], S.qarr)
+    if whole:
+        g.wait_ge(S.wcp, 1)
+        send(prev, T.wl[:], T.wb[:], S.warr)
     if nxt is not None:
         g.wait_ge(S.cpn, 1)
         send(nxt, T.pl[:], T.ps[:], S.parr)
@@ -83,59 +98,72 @@ def rank_program(g, core, T, topo):
         g.wait_ge(S.sent, sent[0])
 
     nb = [b for b in range(KB) if not (ships and b == sb)] if nxt is not None else []
-    half = (len(nb) + 1) // 2
-    own = [(T.kv[:, kcol(b):kcol(b) + P], T.kv[:, vcol(b):vcol(b) + P]) for b in range(KB)]
-    if gets:
-        own.append((T.kvx[:, 0:P], T.kvx[:, P:2 * P]))
-
+    pn = (T.pn0, T.pn1, T.pn2, T.pn3)
+    sns = (S.sn0, S.sn1, S.sn2, S.sn3)
+    rns = (S.rn0, S.rn1, S.rn2, S.rn3)
+    pw, sws, rws = (T.pwa, T.pwb), (S.swa, S.swb), (S.rwa, S.rwb)
     te, ve = g.tensor, g.vector
 
     te.wait_ge(S.kld, 16)
-    if nb:
-        te.wait_ge(S.qarr, NENG)
-        for i, b in enumerate(nb):
-            bank, sem, c = (T.pna, S.sna, i) if i < half else (T.pnb, S.snb, i - half)
-            te.matmul(bank[:, c * QP:(c + 1) * QP], T.kv[:, kcol(b):kcol(b) + P], T.qn[:], True, True).then_inc(sem, 1)
-        te.wait_ge(S.vld, 16)
-        te.wait_ge(S.rna, 1)
-        for i, b in enumerate(nb):
-            if i == half:
-                te.wait_ge(S.rnb, 1)
-            te.matmul(T.pno[:, 0:QP], T.kv[:, vcol(b):vcol(b) + P], T.sn[:, i * QP:(i + 1) * QP],
-                      i == 0, i == len(nb) - 1).then_inc(S.ono, 1)
-    else:
-        te.wait_ge(S.vld, 16)
     te.wait_ge(S.qld, 16)
     if ships:
         te.wait_ge(S.shld, 32)
+    for b in range(KB):
+        h, c = b // HB, b % HB
+        te.matmul(pw[h][:, c * QP:(c + 1) * QP], T.kv[:, kcol(b):kcol(b) + P], T.qs[:], True, True).then_inc(sws[h], 1)
+    te.wait_ge(S.vld, 16)
+    for b in range(KB):
+        if b % HB == 0:
+            te.wait_ge(rws[b // HB], 1)
+        te.matmul(T.pwo[:, 0:QP], T.kv[:, vcol(b):vcol(b) + P], T.sw[:, b * QP:(b + 1) * QP],
+                  b == 0, b == KB - 1 and not gets).then_inc(S.owo, 1)
+    if nb:
+        te.wait_ge(S.qarr, nfrom_next)
+        for i, b in enumerate(nb):
+            te.matmul(pn[i][:, 0:QP], T.kv[:, kcol(b):kcol(b) + P], T.qn[:], True, True).then_inc(sns[i], 1)
+        for i, b in enumerate(nb):
+            te.wait_ge(rns[i], 1)
+            te.matmul(T.pno[:, 0:QP], T.kv[:, vcol(b):vcol(b) + P], T.sn[:, i * QP:(i + 1) * QP],
+                      i == 0, i == len(nb) - 1).then_inc(S.ono, 1)
     if gets:
-        te.wait_ge(S.xarr, NENG)
-    for i, (kb, vb) in enumerate(own):
-        te.matmul(T.pws[:, i * QP:(i + 1) * QP], kb, T.qs[:], True, True).then_inc(S.sws, 1)
-    te.wait_ge(S.rws, 1)
-    for i, (kb, vb) in enumerate(own):
-        te.matmul(T.pwo[:, 0:QP], vb, T.sw[:, i * QP:(i + 1) * QP], i == 0, i == len(own) - 1).then_inc(S.owo, 1)
+        te.wait_ge(S.xarr, nfrom_prev)
+        te.matmul(T.pwa[:, 0:QP], T.kvx[:, 0:P], T.qs[:], True, True).then_inc(S.sxs, 1)
+        te.wait_ge(S.rxs, 1)
+        te.matmul(T.pwo[:, 0:QP], T.kvx[:, P:2 * P], T.sw[:, KB * QP:(KB + 1) * QP], False, True).then_inc(S.owo, 1)
 
     ve.memset(T.zero[:], 0.0).then_inc(S.zs, 1)
     ve.wait_ge(S.zs, 1)
-    if nb:
-        wa, wb = half * QP, (len(nb) - half) * QP
-        ve.wait_ge(S.sna, half)
-        ve.tensor_tensor(T.sn[:, 0:wa], T.pna[:, 0:wa], T.zero[:, 0:wa], AluOpType.max).then_inc(S.rna, 1)
-        ve.wait_ge(S.snb, len(nb) - half)
-        ve.tensor_tensor(T.sn[:, wa:wa + wb], T.pnb[:, 0:wb], T.zero[:, 0:wb], AluOpType.max).then_inc(S.rnb, 1)
-        ve.wait_ge(S.ono, len(nb))
-        ve.tensor_copy(T.ps[:], T.pno[:, 0:QP]).then_inc(S.cpn, 1)
-    ww = len(own) * QP
-    ve.wait_ge(S.sws, len(own))
-    ve.tensor_tensor(T.sw[:, 0:ww], T.pws[:, 0:ww], T.zero[:, 0:ww], AluOpType.max).then_inc(S.rws, 1)
-    ve.wait_ge(S.owo, len(own))
-    if prev is not None:
-        ve.wait_ge(S.parr, NENG)
-        ve.tensor_tensor(T.yb[:], T.pwo[:, 0:QP], T.pl[:], AluOpType.add).then_inc(S.fin, 1)
-    else:
+    for h in range(2):
+        ve.wait_ge(sws[h], HB)
+        ve.tensor_tensor(T.sw[:, h * HW:(h + 1) * HW], pw[h][:, 0:HW], T.zero[:], AluOpType.max).then_inc(rws[h], 1)
+    if whole:
+        ve.wait_ge(S.owo, KB)
+        ve.tensor_copy(T.wb[:], T.pwo[:, 0:QP]).then_inc(S.wcp, 1)
+    if prev is None:
+        ve.wait_ge(S.owo, KB)
         ve.tensor_copy(T.yb[:], T.pwo[:, 0:QP]).then_inc(S.fin, 1)
+    if nb:
+        for i in range(len(nb)):
+            ve.wait_ge(sns[i], 1)
+            ve.tensor_tensor(T.sn[:, i * QP:(i + 1) * QP], pn[i][:, 0:QP], T.zero[:, 0:QP], AluOpType.max).then_inc(rns[i], 1)
+        if gives:
+            ve.wait_ge(S.warr, nfrom_next)
+        ve.wait_ge(S.ono, len(nb))
+        if gives:
+            ve.tensor_tensor(T.ps[:], T.pno[:, 0:QP], T.wl[:], AluOpType.add).then_inc(S.cpn, 1)
+        else:
+            ve.tensor_copy(T.ps[:], T.pno[:, 0:QP]).then_inc(S.cpn, 1)
+    if gets:
+        ve.wait_ge(S.sxs, 1)
+        ve.tensor_tensor(T.sw[:, KB * QP:(KB + 1) * QP], T.pwa[:, 0:QP], T.zero[:, 0:QP], AluOpType.max).then_inc(S.rxs, 1)
+        ve.wait_ge(S.owo, KB + 1)
+        ve.wait_ge(S.parr, nfrom_prev)
+        ve.tensor_tensor(T.yb[:], T.pwo[:, 0:QP], T.pl[:], AluOpType.add).then_inc(S.fin, 1)
 
-    g.sync.wait_ge(S.fin, 1)
-    g.sync.dma_start(T.y[:], T.yb[:]).then_inc(S.yst, 16)
+    if whole:
+        g.sync.wait_ge(S.parr, nfrom_prev)
+        g.sync.dma_start(T.y[:], T.pl[:]).then_inc(S.yst, 16)
+    else:
+        g.sync.wait_ge(S.fin, 1)
+        g.sync.dma_start(T.y[:], T.yb[:]).then_inc(S.yst, 16)
     g.sync.wait_ge(S.yst, 16)

from concourse.mybir import AluOpType

P = 128
KB, QP = 4, 64
KW = KB * P
HB = KB // 2
HW = HB * QP

SCRATCH = {
    "qs":   ("sbuf", [P, QP], "bfloat16"),
    "kv":   ("sbuf", [P, 2 * KW], "bfloat16"),
    "qn":   ("sbuf", [P, QP], "bfloat16"),
    "wl":   ("sbuf", [P, QP], "bfloat16"),
    "kvx":  ("sbuf", [P, 2 * P], "bfloat16"),
    "pl":   ("sbuf", [P, QP], "bfloat16"),
    "ps":   ("sbuf", [P, QP], "bfloat16"),
    "wb":   ("sbuf", [P, QP], "bfloat16"),
    "zero": ("sbuf", [P, HW], "float32"),
    "sn":   ("sbuf", [P, KB * QP], "bfloat16"),
    "sw":   ("sbuf", [P, (KB + 1) * QP], "bfloat16"),
    "yb":   ("sbuf", [P, QP], "bfloat16"),
    "pn0":  ("psum", [P, 512], "float32"),
    "pn1":  ("psum", [P, 512], "float32"),
    "pn2":  ("psum", [P, 512], "float32"),
    "pn3":  ("psum", [P, 512], "float32"),
    "pno":  ("psum", [P, 512], "float32"),
    "pwa":  ("psum", [P, 512], "float32"),
    "pwb":  ("psum", [P, 512], "float32"),
    "pwo":  ("psum", [P, 512], "float32"),
}
SEMAPHORES = ["qld", "qiss", "kld", "vld", "shld", "qarr", "warr", "xarr", "parr", "sent", "zs",
              "sn0", "sn1", "sn2", "sn3", "rn0", "rn1", "rn2", "rn3", "ono", "cpn", "wcp",
              "swa", "swb", "rwa", "rwb", "sxs", "rxs", "owo", "fin", "yst"]


def _count(mask):
    return sum((mask >> i) & 1 for i in range(mask.bit_length()))


def rank_program(g, core, T, topo):
    r = T.rank_of(core)
    if r is None:
        return
    cores = T.cores
    prev = cores[r - 1] if r > 0 else None
    nxt = cores[r + 1] if r + 1 < len(cores) else None
    S = T.sem
    ships = prev is None and nxt is not None
    gets = prev is not None and T.rank_of(prev) == 0
    whole = prev is not None and not gets
    gives = nxt is not None and not ships
    sb = KB - 1

    def kcol(b):
        return P * b

    def vcol(b):
        return KW + P * ((b + 1) % KB) if ships else KW + P * b

    sent = [0]

    def send(dst, out_ap, in_ap, sem):
        rid, pid = topo.addr(dst, core)
        mask = topo.mask(core, dst)
        g.remote_dma(out_ap=out_ap, in_ap=in_ap, remote_sem=sem, local_sem=S.sent, pid=pid, routing_id=rid,
                     dma_engine_mask=mask)
        sent[0] += _count(mask)

    nfrom_prev = _count(topo.mask(prev, core)) if prev is not None else 0
    nfrom_next = _count(topo.mask(nxt, core)) if nxt is not None else 0

    if ships:
        g.sync.dma_start(T.kv[:, kcol(sb):kcol(sb) + P], T.k[:, P * sb:P * sb + P]).then_inc(S.shld, 16)
        g.scalar.dma_start(T.kv[:, vcol(sb):vcol(sb) + P], T.v[:, P * sb:P * sb + P]).then_inc(S.shld, 16)
        g.sync.dma_start(T.kv[:, 0:P * sb], T.k[:, 0:P * sb]).then_inc(S.kld, 16)
        g.scalar.dma_start(T.kv[:, vcol(0):vcol(0) + P * sb], T.v[:, 0:P * sb]).then_inc(S.vld, 16)
        g.sync.dma_start(T.qs[:], T.q[:]).then_inc(S.qld, 16)
    else:
        g.sync.dma_start(T.qs[:], T.q[:]).then_inc(S.qld, 16)
        g.sync.sem_inc(S.qiss, 1)
        g.sync.dma_start(T.kv[:, 0:KW], T.k[:]).then_inc(S.kld, 16)
        g.scalar.wait_ge(S.qiss, 1)
        g.scalar.dma_start(T.kv[:, KW:2 * KW], T.v[:]).then_inc(S.vld, 16)

    if ships:
        g.wait_ge(S.shld, 32)
        send(nxt, T.kvx[:], T.kv[:, kcol(sb):kcol(sb) + 2 * P], S.xarr)
    if prev is not None:
        g.wait_ge(S.qld, 16)
        send(prev, T.qn[:], T.qs[:], S.qarr)
    if whole:
        g.wait_ge(S.wcp, 1)
        send(prev, T.wl[:], T.wb[:], S.warr)
    if nxt is not None:
        g.wait_ge(S.cpn, 1)
        send(nxt, T.pl[:], T.ps[:], S.parr)
    if sent[0]:
        g.wait_ge(S.sent, sent[0])

    nb = [b for b in range(KB) if not (ships and b == sb)] if nxt is not None else []
    pn = (T.pn0, T.pn1, T.pn2, T.pn3)
    sns = (S.sn0, S.sn1, S.sn2, S.sn3)
    rns = (S.rn0, S.rn1, S.rn2, S.rn3)
    pw, sws, rws = (T.pwa, T.pwb), (S.swa, S.swb), (S.rwa, S.rwb)
    te, ve = g.tensor, g.vector

    te.wait_ge(S.kld, 16)
    te.wait_ge(S.qld, 16)
    if ships:
        te.wait_ge(S.shld, 32)
    for b in range(KB):
        h, c = b // HB, b % HB
        te.matmul(pw[h][:, c * QP:(c + 1) * QP], T.kv[:, kcol(b):kcol(b) + P], T.qs[:], True, True).then_inc(sws[h], 1)
    te.wait_ge(S.vld, 16)
    for b in range(KB):
        if b % HB == 0:
            te.wait_ge(rws[b // HB], 1)
        te.matmul(T.pwo[:, 0:QP], T.kv[:, vcol(b):vcol(b) + P], T.sw[:, b * QP:(b + 1) * QP],
                  b == 0, b == KB - 1 and not gets).then_inc(S.owo, 1)
    if nb:
        te.wait_ge(S.qarr, nfrom_next)
        for i, b in enumerate(nb):
            te.matmul(pn[i][:, 0:QP], T.kv[:, kcol(b):kcol(b) + P], T.qn[:], True, True).then_inc(sns[i], 1)
        for i, b in enumerate(nb):
            te.wait_ge(rns[i], 1)
            te.matmul(T.pno[:, 0:QP], T.kv[:, vcol(b):vcol(b) + P], T.sn[:, i * QP:(i + 1) * QP],
                      i == 0, i == len(nb) - 1).then_inc(S.ono, 1)
    if gets:
        te.wait_ge(S.xarr, nfrom_prev)
        te.matmul(T.pwa[:, 0:QP], T.kvx[:, 0:P], T.qs[:], True, True).then_inc(S.sxs, 1)
        te.wait_ge(S.rxs, 1)
        te.matmul(T.pwo[:, 0:QP], T.kvx[:, P:2 * P], T.sw[:, KB * QP:(KB + 1) * QP], False, True).then_inc(S.owo, 1)

    ve.memset(T.zero[:], 0.0).then_inc(S.zs, 1)
    ve.wait_ge(S.zs, 1)
    for h in range(2):
        ve.wait_ge(sws[h], HB)
        ve.tensor_tensor(T.sw[:, h * HW:(h + 1) * HW], pw[h][:, 0:HW], T.zero[:], AluOpType.max).then_inc(rws[h], 1)
    if whole:
        ve.wait_ge(S.owo, KB)
        ve.tensor_copy(T.wb[:], T.pwo[:, 0:QP]).then_inc(S.wcp, 1)
    if prev is None:
        ve.wait_ge(S.owo, KB)
        ve.tensor_copy(T.yb[:], T.pwo[:, 0:QP]).then_inc(S.fin, 1)
    if nb:
        for i in range(len(nb)):
            ve.wait_ge(sns[i], 1)
            ve.tensor_tensor(T.sn[:, i * QP:(i + 1) * QP], pn[i][:, 0:QP], T.zero[:, 0:QP], AluOpType.max).then_inc(rns[i], 1)
        if gives:
            ve.wait_ge(S.warr, nfrom_next)
        ve.wait_ge(S.ono, len(nb))
        if gives:
            ve.tensor_tensor(T.ps[:], T.pno[:, 0:QP], T.wl[:], AluOpType.add).then_inc(S.cpn, 1)
        else:
            ve.tensor_copy(T.ps[:], T.pno[:, 0:QP]).then_inc(S.cpn, 1)
    if gets:
        ve.wait_ge(S.sxs, 1)
        ve.tensor_tensor(T.sw[:, KB * QP:(KB + 1) * QP], T.pwa[:, 0:QP], T.zero[:, 0:QP], AluOpType.max).then_inc(S.rxs, 1)
        ve.wait_ge(S.owo, KB + 1)
        ve.wait_ge(S.parr, nfrom_prev)
        ve.tensor_tensor(T.yb[:], T.pwo[:, 0:QP], T.pl[:], AluOpType.add).then_inc(S.fin, 1)

    if whole:
        g.sync.wait_ge(S.parr, nfrom_prev)
        g.sync.dma_start(T.y[:], T.pl[:]).then_inc(S.yst, 16)
    else:
        g.sync.wait_ge(S.fin, 1)
        g.sync.dma_start(T.y[:], T.yb[:]).then_inc(S.yst, 16)
    g.sync.wait_ge(S.yst, 16)
